import numpy as np, ml_dtypes
CORES = [16,18,20,22]
N = 4
BF = ml_dtypes.bfloat16
def gentries(a):
    return np.ascontiguousarray(a.reshape(8, 16, -1).transpose(0, 2, 1)).reshape(8, -1)
def gtable(e):
    e = np.asarray(e); return np.ascontiguousarray(e.reshape(8, -1, 16).transpose(0, 2, 1)).reshape(128, -1).astype(np.int32)
S, P, CAP, R = 4096, 1024, 320, 6
LEAST = -(-P // CAP)
def counts(rng, m):
    w = np.repeat(np.exp2(rng.integers(-2, 3, m)), CAP - 1); slot = np.argsort(-rng.random(m * (CAP - 1)) * w)[:P - m] // (CAP - 1)
    return np.bincount(slot, minlength=R) + (np.arange(R) < m)
def fountain(rng, cnt, src, e=1, full=False):
    pk = np.zeros((N, 128, P), np.float32); nb = np.zeros((N, 8, 4, P), np.int64)
    def pick(n):
        return np.minimum((rng.random(S) ** e * n).astype(np.int64), n - 1)
    for g in range(8):
        rd = np.concatenate([rng.permutation(np.repeat(np.arange(R), cnt[q, g])) for q in range(N)])
        at = np.argsort(rd, kind="stable"); t = rd[at]; end = np.concatenate([[0], np.cumsum(np.bincount(rd, minlength=R))])
        hi = end[t]; lo = end[np.maximum(t - 1, 0)]; most = np.maximum(hi, 3)
        a = lo + pick(np.maximum(hi - lo, 1))
        b = pick(most - 1); b = b + (b >= a)
        c = pick(most - 2); c = c + (c >= np.minimum(a, b)); c = c + (c >= np.maximum(a, b))
        if e > 1:
            o = np.concatenate([[S - 1, 0], 1 + rng.permutation(S - 2)])
        else:
            o = rng.permutation(S)
        deg = np.where(t == 0, 0, 3 if full else rng.integers(1, 4, S))
        row = np.stack([o, np.where(deg > 0, o[a], S), np.where(deg > 1, o[b], S), np.where(deg > 2, o[c], S)], axis=1)
        four = np.zeros((S, 4), np.int64); four[at] = rng.permuted(row, axis=1)
        v = np.concatenate([src[g], np.zeros((16, 1), np.int64)], axis=1)
        pk[:, 16 * g:16 * g + 16] = (np.sum(v[:, four], axis=2) & 255).reshape(16, N, P).transpose(1, 0, 2)
        nb[:, g] = four.reshape(N, P, 4).transpose(0, 2, 1)
    return {"packets": pk.astype(BF), "nb": np.stack([gtable(nb[q].reshape(8, 4 * P)) for q in range(N)])}
def anycounts(rng):
    return np.stack([np.stack([counts(rng, R) for g in range(8)]) for q in range(N)])
def setup_inputs(rng):
    return fountain(rng, anycounts(rng), rng.integers(0, 256, (8, 16, S)))
def setup_inputs_caps(rng):
    cnt = anycounts(rng); early = np.zeros(R, np.int64); early[:P // CAP] = CAP; early[P // CAP] = P % CAP
    for g in range(8):
        q = rng.permutation(N); cnt[q[0], g] = early; cnt[q[1], g] = early[::-1]
    cnt[:, rng.integers(0, 8)] = early
    return fountain(rng, cnt, rng.integers(0, 256, (8, 16, S)))
def setup_inputs_short(rng):
    m = rng.permutation(LEAST + np.arange(8) % (R - LEAST + 1)); cnt = np.stack([np.stack([counts(rng, m[g]) for g in range(8)]) for q in range(N)])
    return fountain(rng, cnt, rng.integers(0, 256, (8, 16, S)))
def setup_inputs_hubs(rng):
    return fountain(rng, anycounts(rng), rng.integers(236, 256, (8, 16, S)), e=8, full=True)
def setup_inputs_spread(rng):
    src = np.floor(rng.random((8, 16, S)) * np.exp2(rng.integers(0, 9, (8, 1, S)))) * (rng.random((8, 1, S)) > 0.0625)
    return fountain(rng, anycounts(rng), src.astype(np.int64))
def check_inputs(d):
    bad = []; x = d["packets"].astype(np.float32)
    if not ((x >= 0) & (x <= 255) & (x == np.floor(x))).all():
        bad.append("packets")
    if d["nb"].min() < 0 or d["nb"].max() > S:
        return bad + ["nb"]
    nbr = np.concatenate([gentries(d["nb"][q]).reshape(8, 4, P) for q in range(N)], axis=2).astype(np.int64)
    z = np.sort(nbr, axis=1)
    if ((z[:, 1:] == z[:, :-1]) & (z[:, 1:] < S)).any():
        bad.append("neighbours differ")
    known = np.zeros((8, S + 1), bool); known[:, S] = True; over = False
    for t in range(R):
        for g in range(8):
            un = ~known[g][nbr[g]]; j = np.nonzero(np.sum(un, axis=0) == 1)[0]
            over = over or np.bincount(j // P, minlength=N).max() > CAP
            known[g, np.sum(np.where(un[:, j], nbr[g][:, j], 0), axis=0)] = True
    if over:
        bad.append("cap")
    if not known.all():
        bad.append("all released")
    return bad
def reference(packets, nb):
    nbr = np.concatenate([gentries(nb[q]).reshape(8, 4, P) for q in range(N)], axis=2).astype(np.int64)
    pk = np.concatenate([packets[q].astype(np.float32).reshape(8, 16, P) for q in range(N)], axis=2).astype(np.int64)
    v = np.zeros((8, 16, S + 1), np.int64); known = np.zeros((8, S + 1), bool); known[:, S] = True
    w = np.zeros((8, S + 1), np.int64)
    for t in range(1, R + 1):
        for g in range(8):
            un = ~known[g][nbr[g]]; j = np.nonzero(np.sum(un, axis=0) == 1)[0]; p = nbr[g][:, j]
            s = np.sum(np.where(un[:, j], p, 0), axis=0)
            new = (pk[g][:, j] - np.sum(v[g][:, p], axis=1)) & 255
            v[g][:, s] = new; w[g, s] = t; known[g, s] = True
    y = v[:, :, :S].reshape(128, N, P).transpose(1, 0, 2); u = w[:, :S].reshape(8, N, P).transpose(1, 0, 2)
    return {"y": np.ascontiguousarray(y).astype(np.float32), "rounds": np.ascontiguousarray(u).astype(np.float32)}

@@ -1,0 +1,393 @@
+from concourse.bass import DstId, RemoteDMATransfer
+from concourse.mybir import AluOpType as ALU, ActivationFunctionType as ACT
+
+S, P, R = 4096, 1024, 6
+U = 49152.0
+BASE = 6144
+HI = BASE + S
+WIN = HI + P
+BIG = 16384.0
+EDGES = [0, 16, 32, 48, 64]
+PIECES = [(3, 256), (7, 256), (0, 512), (4, 512), (1, 512), (5, 512), (2, 512), (6, 512), (3, 256), (7, 256)]
+
+SCRATCH = {
+    "d_nb": ("dram", [4, 128, 64], "int32"),
+    "l_nb": ("dram", [4, 128, 64], "int32"),
+    "d_pk": ("dram", [4, 128, 256], "bfloat16"),
+    "l_pk": ("dram", [4, 128, 256], "bfloat16"),
+    "l_y": ("dram", [4, 128, 256], "float32"),
+    "nbs": ("sbuf", [128, 256], "int32"),
+    "pk": ("sbuf", [128, 1024], "bfloat16"),
+    "off": ("sbuf", [128, 256], "uint16"),
+    "soff": ("sbuf", [128, 64], "uint16"),
+    "av": ("sbuf", [128, 320], "float32"),
+    "mm": ("sbuf", [128, 320], "float32"),
+    "lh": ("sbuf", [128, 320], "float32"),
+    "zz": ("sbuf", [128, 320], "float32"),
+    "cw": ("sbuf", [128, 160], "bfloat16"),
+    "tab": ("sbuf", [128, WIN], "bfloat16"),
+    "tt": ("sbuf", [128, S + 16], "bfloat16"),
+    "gg": ("sbuf", [128, 1024, 4], "bfloat16"),
+    "qq": ("sbuf", [128, 1024], "bfloat16"),
+    "rr": ("sbuf", [128, 1024], "bfloat16"),
+    "di": ("sbuf", [128, 128], "int32"),
+    "dj": ("sbuf", [128, 128], "int32"),
+    "dk": ("sbuf", [128, 16], "int32"),
+    "c16": ("sbuf", [128, 64], "float32"),
+    "pmi": ("sbuf", [128, 4], "int32"),
+    "pmj": ("sbuf", [128, 4], "int32"),
+    "pmf": ("sbuf", [128, 4], "float32"),
+    "m16": ("sbuf", [128, 16], "float32"),
+    "eye": ("sbuf", [128, 128], "bfloat16"),
+    "neg": ("sbuf", [128, 128], "bfloat16"),
+    "cmb": ("sbuf", [128, 128], "bfloat16"),
+    "sel": ("sbuf", [128, 2048], "bfloat16"),
+    "fin": ("sbuf", [128, 512], "bfloat16"),
+    "rt": ("sbuf", [128, 320], "bfloat16"),
+    "sg": ("sbuf", [128, 320], "bfloat16"),
+    "ro": ("sbuf", [128, 64], "float32"),
+    "rl": ("sbuf", [128, 256], "float32"),
+    "yo": ("sbuf", [128, 1024], "float32"),
+}
+for _b in range(8):
+    SCRATCH["b%d" % _b] = ("psum", [128, 512] if _b < 4 else [128, 64, 8], "float32")
+
+SEMAPHORES = ["sv", "sa", "sp", "sg", "st_nb", "st_pk", "own_nb", "own_pk", "ar_nb", "ar_pk", "re_nb", "re_pk", "rd",
+              "ar_r", "ar_y0", "ar_y1", "ar_y2", "ar_y3", "loc", "out"]
+
+ORDER_V = ["g00", "g02", "g10", "g12", "g20", "g22", "b0", "q0", "c0", "r0", "d0", "b1", "s0", "c1", "r1", "d1", "b2", "s1",
+           "c2", "r2", "d2", "b3", "s2", "c3", "r3", "d3", "s3"]
+ORDER_A = ["g01", "g03", "g11", "g13", "g21", "a0", "g23", "g30", "a1", "g31", "q1", "g32", "a2", "g33", "q2", "a3", "q3"]
+ORDER_P = ["w0", "x0", "w1", "x1", "w2", "x2", "w3", "x3"]
+
+
+def rank_program(g, core, T, topo):
+    rank = T.rank_of(core)
+    if rank is None:
+        return
+    cores = list(T.cores)
+    n = len(cores)
+    Q = {"V": g.vector, "A": g.scalar, "P": g.tensor, "G": g, "Y": g.sync}
+    own = {"V": "sv", "A": "sa", "P": "sp", "G": "sg"}
+    clock = {k: {} for k in Q}
+    total = {}
+    last_w, readers = {}, {}
+
+    def wait(q, ev):
+        sem, cnt, seen = ev
+        if clock[q].get(sem, 0) >= cnt:
+            return
+        Q[q].wait_ge(T.sem[sem], cnt)
+        clock[q][sem] = cnt
+        for k, v in seen.items():
+            if clock[q].get(k, 0) < v:
+                clock[q][k] = v
+
+    def deps(reads, writes):
+        evs = []
+        for x in list(reads) + list(writes):
+            if x in last_w:
+                evs.append(last_w[x])
+        for x in writes:
+            evs.extend(readers.get(x, []))
+        best = {}
+        for e in evs:
+            if e[0] not in best or best[e[0]][1] < e[1]:
+                best[e[0]] = e
+        return sorted(best.values(), key=lambda e: -len(e[2]))
+
+    def op(q, fn, reads=(), writes=(), sem=None, inc=1, after=()):
+        for e in list(after) + deps(reads, writes):
+            wait(q, e)
+        ins = fn()
+        if inc == 0:
+            return None
+        sem = sem or own[q]
+        ins.then_inc(T.sem[sem], inc)
+        total[sem] = total.get(sem, 0) + inc
+        ev = (sem, total[sem], dict(clock[q]))
+        for x in reads:
+            readers.setdefault(x, []).append(ev)
+        for x in writes:
+            last_w[x] = ev
+            readers[x] = []
+        return ev
+
+    def dma(q, out, in_, sem, reads=(), writes=(), after=()):
+        return op(q, lambda: Q[q].dma_start(out, in_), reads, writes, sem=sem, inc=16, after=after)
+
+    V, A, PE = g.vector, g.scalar, g.tensor
+    bank = [T["b%d" % b] for b in range(8)]
+
+    def dests_of(q):
+        o = [u for u in range(n) if u != q]
+        return [u for u in o if topo.die(cores[u]) != topo.die(cores[q])] + \
+               [u for u in o if topo.die(cores[u]) == topo.die(cores[q])]
+
+    others = [u for u in range(n) if u != rank]
+    dests = dests_of(rank)
+    eng = topo.engines(core, cores[others[0]])
+
+    def bits(lst):
+        m = 0
+        for e in lst:
+            m |= 1 << e
+        return m
+
+    def dst(u):
+        rid, pid, _ = topo.addr(cores[u])
+        return DstId(rid=rid, pnc=pid)
+
+    ev_e, od_e = eng[0::2], eng[1::2]
+    nb_eng = [ev_e[0:2], ev_e[2:4], od_e[0:2]]
+    pk_eng = [ev_e[0:2] + ev_e[4:6], ev_e[2:4] + ev_e[6:8], od_e[0:2] + od_e[4:6]]
+    r_eng = od_e[2:4] + od_e[6:8]
+    loc = [0]
+
+    def arrivals(table):
+        return sum(len(table[dests_of(q).index(rank)]) for q in others)
+
+    e_st_nb = dma("Y", T.d_nb[:], T.nb[:], "st_nb")
+    e_st_pk = dma("A", T.d_pk[:], T.packets[:], "st_pk")
+    e_own_nb = dma("Y", T.l_nb[rank], T.nb[32 * rank:32 * rank + 32, :], "own_nb")
+    e_own_pk = dma("A", T.l_pk[rank], T.packets[32 * rank:32 * rank + 32, :], "own_pk")
+
+    op("G", lambda: g.iota(T.di[:], [[-1, 128]], 128, 1), writes=["di"])
+    op("G", lambda: g.iota(T.c16[:], [[16, 64]], 0, 0, allow_small_or_imprecise_dtypes=True), writes=["c16"])
+    op("G", lambda: g.iota(T.pmi[:], [[0, 4]], 0, 1), writes=["pmi"])
+
+    wait("G", e_st_nb)
+    g.remote_dma_fused([RemoteDMATransfer(dst_ids=[dst(u)], dma_engine_mask=bits(nb_eng[k]), remote_sem=T.sem.ar_nb,
+                                          src=T.d_nb[u], dst=T.l_nb[rank]) for k, u in enumerate(dests)], local_sem=T.sem.loc)
+    loc[0] += sum(len(x) for x in nb_eng)
+    wait("G", e_st_pk)
+    g.remote_dma_fused([RemoteDMATransfer(dst_ids=[dst(u)], dma_engine_mask=bits(pk_eng[k]), remote_sem=T.sem.ar_pk,
+                                          src=T.d_pk[u], dst=T.l_pk[rank]) for k, u in enumerate(dests)], local_sem=T.sem.loc)
+    loc[0] += sum(len(x) for x in pk_eng)
+
+    dma("Y", T.nbs[:], T.l_nb[:], "re_nb", writes=["nbs"], after=[e_own_nb, ("ar_nb", arrivals(nb_eng), {})])
+    dma("A", T.pk[:], T.l_pk[:], "re_pk", writes=["pk"], after=[e_own_pk, ("ar_pk", arrivals(pk_eng), {})])
+
+    op("V", lambda: V.memset(T.tab[:, BASE:HI], -U), writes=["tab"])
+    op("V", lambda: V.memset(T.tt[:, S:S + 16], 0.0), writes=["ttz"])
+    op("V", lambda: V.memset(T.av[:, 0::5], BIG), writes=["av4"])
+    op("V", lambda: V.memset(bank[1][:, 0:320:5], BIG), writes=["w1_4"])
+    op("V", lambda: V.memset(T.cw[:], 0.0), writes=["cw"])
+    op("V", lambda: V.memset(T.fin[:], 0.0), writes=["fin"])
+    op("V", lambda: V.tensor_scalar(T.eye[:], T.di[:], 128, None, ALU.is_equal), ["di"], ["eye"])
+    op("V", lambda: V.tensor_scalar(T.neg[:], T.di[:], 128, -1.0, ALU.is_equal, ALU.mult), ["di"], ["neg"])
+    op("V", lambda: V.tensor_scalar(T.dj[:], T.di[:], 31, None, ALU.bitwise_and), ["di"], ["dj"])
+    op("V", lambda: V.tensor_scalar(T.dk[:], T.di[:, 0:16], 15, None, ALU.bitwise_and), ["di"], ["dk"])
+    op("V", lambda: V.tensor_scalar(T.pmj[:], T.pmi[:], 15, None, ALU.bitwise_and), ["pmi"], ["pmj"])
+    op("V", lambda: V.memset(T.cw[:, 0::5], -U), writes=["cw"])
+    op("V", lambda: V.tensor_scalar(T.cmb[:], T.dj[:], 0, None, ALU.is_equal), ["dj"], ["cmb"])
+    op("V", lambda: V.tensor_scalar(T.m16[:], T.dk[:], 0, None, ALU.is_equal), ["dk"], ["m16"])
+    op("V", lambda: V.tensor_copy(T.pmf[:], T.pmj[:]), ["pmj"], ["pmf"])
+    for w in range(4):
+        op("V", lambda: V.tensor_copy(T.fin[:, 128 * w + w:128 * w + 128:4], T.cmb[:, 0:32]), ["cmb", "fin"], ["fin%d" % w])
+    op("V", lambda: V.tensor_scalar(T.lh[:, 0::5], T.c16[:], T.pmf[:, 0:1], None, ALU.add), ["c16", "pmf"], ["lh0"])
+    for k in range(1, 5):
+        op("V", lambda: V.tensor_scalar(T.lh[:, k::5], T.c16[:], T.pmf[:, 0:1], float(HI), ALU.add, ALU.add),
+           ["c16", "pmf"], ["lh%d" % k])
+    op("V", lambda: V.tensor_scalar(bank[0][:, 0:64], T.lh[:, 0::5], -1.0, float(BASE), ALU.mult, ALU.add), ["lh0"], ["B0"])
+    for i in range(16):
+        op("V", lambda: V.tensor_scalar(T.sel[:, 128 * i:128 * i + 128], T.eye[:], T.m16[:, i:i + 1], None, ALU.mult),
+           ["eye", "m16"], ["sel%d" % i])
+    LH = ["lh%d" % k for k in range(5)]
+    SEL = ["sel%d" % i for i in range(16)]
+    TT = ["tt%d" % b for b in range(len(PIECES))] + ["ttz"]
+    AV = ["av%d" % k for k in range(5)]
+
+    for k in range(4):
+        op("V", lambda: V.tensor_scalar(bank[1][:, k + 1:320:5], T.nbs[:, 64 * k:64 * k + 64], -float(S), -BIG, ALU.add, ALU.mult),
+           ["nbs"], ["w1_%d" % k])
+    for k in range(4):
+        op("V", lambda: V.tensor_tensor(T.av[:, k + 1::5], T.nbs[:, 64 * k:64 * k + 64], bank[0][:, 0:64], ALU.add),
+           ["nbs", "B0"], ["av%d" % k])
+    MM = ["mm%d" % c for c in range(4)]
+    op("V", lambda: V.tensor_tensor(T.mm[:], bank[1][:, 0:320], T.av[:], ALU.min),
+       AV + ["w1_%d" % k for k in range(5)], MM + ["B0", "B1"])
+    op("V", lambda: V.tensor_tensor_scan(T.zz[:], T.mm[:], T.lh[:], 0.0, ALU.add, ALU.min), MM + LH,
+       ["zz%d" % c for c in range(4)])
+    op("V", lambda: V.tensor_copy(T.soff[:], T.zz[:, 4::5]), ["zz%d" % c for c in range(4)], ["so%d" % c for c in range(4)])
+    op("V", lambda: V.tensor_copy(T.tab[:, 0:WIN].indirect(T.soff[:, 0:64]), T.pk[:]),
+       ["pk"] + ["so%d" % c for c in range(4)], ["tab"])
+    op("V", lambda: V.tensor_copy(T.off[:], T.nbs[:]), ["nbs"], ["off"])
+
+    def combine(t):
+        start = [sum(w for _, w in PIECES[:k]) for k in range(len(PIECES))]
+
+        def region(k):
+            b, w = PIECES[k]
+            return bank[b][:, 0:w] if b < 4 else bank[b][:, 0:w // 8, :]
+
+        def add(k):
+            a = BASE + start[k]
+            op("P", lambda: PE.matmul(region(k), T.cmb[:], T.tab[:, a:a + PIECES[k][1]], True, True),
+               ["tab", "cmb"], ["B%d" % PIECES[k][0]])
+
+        def move(k):
+            out = T.tt[:, start[k]:start[k] + PIECES[k][1]]
+            if k % 2 == 0:
+                op("V", lambda: V.tensor_scalar(out, region(k), 3 * U, None, ALU.add), [], ["B%d" % PIECES[k][0], "tt%d" % k])
+            else:
+                op("A", lambda: A.activation(out, region(k), ACT.Identity, bias=3 * U), [], ["B%d" % PIECES[k][0], "tt%d" % k])
+
+        for k in range(8):
+            add(k)
+        move(0)
+        move(1)
+        add(8)
+        add(9)
+        for k in range(2, 10):
+            move(k)
+        for c in range(4):
+            c0, c1 = EDGES[c], EDGES[c + 1]
+            op("P", lambda: PE.matmul(bank[4 + c][:, 0:c1 - c0, 0:5], T.eye[:], T.cw[:, 0:5 * (c1 - c0)], True, False),
+               ["cw", "eye"], ["B%d" % (4 + c)], inc=0)
+            op("P", lambda: PE.matmul(bank[c][:, 0:16 * (c1 - c0)], T.eye[:], T.pk[:, 16 * c0:16 * c1], True, False),
+               ["pk", "eye"], ["B%d" % c], inc=0)
+        for gl in range(2):
+            dma("Y", T.rt[64 * gl:64 * gl + 64, 64 * (t - 1):64 * t], T.tt[16 * gl:16 * gl + 1, 0:S], "rd",
+                reads=TT, writes=["rt%d" % gl])
+        both = last_w["rt1"]
+        last_w["rt0"] = both
+        for x in TT:
+            readers[x] = [e for e in readers[x] if e[0] != "rd"] + [both]
+
+    def step(q, name):
+        kind, c = name[0], int(name[1])
+        c0, c1 = EDGES[c], EDGES[c + 1]
+        m = c1 - c0
+        X, W = bank[c][:, 0:16 * m], bank[4 + c]
+        bx, bw = "B%d" % c, "B%d" % (4 + c)
+        gc = ["g%d%d" % (c, k) for k in range(4)]
+        cols = slice(16 * c0, 16 * c1)
+        pc = slice(c0, c1)
+        p5 = slice(5 * c0, 5 * c1)
+        W5 = W[:, 0:m, 0:5]
+        if kind == "g":
+            k = int(name[2])
+            src = T.tt[:, 0:S + 16].indirect(T.off[:, 64 * k + c0:64 * k + c1])
+            if q == "V":
+                op(q, lambda: V.tensor_copy(T.gg[:, cols, k], src), TT + ["off"], [name])
+            else:
+                op(q, lambda: A.activation(T.gg[:, cols, k], src, ACT.Copy), TT + ["off"], [name])
+        elif kind == "w":
+            def f():
+                for i in range(16):
+                    ins = PE.matmul(W[:, 0:m, 1:5], T.sel[:, 128 * i:128 * i + 128], T.gg[:, 16 * c0 + i:16 * c1:16, :],
+                                    False, i == 15)
+                return ins
+            op(q, f, gc + SEL, [bw])
+        elif kind == "x":
+            def f():
+                for k in range(4):
+                    ins = PE.matmul(X, T.neg[:], T.gg[:, cols, k], False, k == 3)
+                return ins
+            op(q, f, gc + ["neg"], [bx])
+        elif kind == "a":
+            if q == "V":
+                op(q, lambda: V.tensor_scalar(W5, W5, -1.0, 0.0, ALU.mult, ALU.max), [], [bw])
+            else:
+                op(q, lambda: A.activation(W5, W5, ACT.Relu, scale=-1.0), [], [bw])
+        elif kind == "b":
+            op(q, lambda: V.tensor_tensor(T.mm[:, p5], W5, T.av[:, p5], ALU.min), AV, [bw, "mm%d" % c])
+        elif kind == "c":
+            op(q, lambda: V.tensor_tensor_scan(T.zz[:, p5], T.mm[:, p5], T.lh[:, p5], 0.0, ALU.add, ALU.min),
+               ["mm%d" % c] + LH, ["zz%d" % c])
+        elif kind == "d":
+            op(q, lambda: V.tensor_copy(T.soff[:, pc], T.zz[:, 5 * c0 + 4:5 * c1:5]), ["zz%d" % c], ["so%d" % c])
+        elif kind == "q":
+            if q == "V":
+                op(q, lambda: V.tensor_scalar(T.qq[:, cols], X, -127.5, None, ALU.add), [], [bx, "q%d" % c])
+            else:
+                op(q, lambda: A.activation(T.qq[:, cols], X, ACT.Identity, bias=-127.5), [], [bx, "q%d" % c])
+        elif kind == "r":
+            op(q, lambda: V.tensor_tensor(T.rr[:, cols], X, T.qq[:, cols], ALU.subtract), ["q%d" % c], [bx, "r%d" % c])
+        elif kind == "s":
+            op(q, lambda: V.tensor_copy(T.tab[:, 0:WIN].indirect(T.soff[:, pc]), T.rr[:, cols]),
+               ["r%d" % c, "so%d" % c], ["tab"])
+        elif kind == "t":
+            op(q, lambda: A.activation(T.sg[:], T.rt[:], ACT.Sign, bias=0.5), ["rt0", "rt1"], ["sg"])
+        elif kind == "u":
+            def f():
+                for t in range(5):
+                    ins = PE.matmul(W[:, 32:40, :], T.eye[:], T.sg[:, 64 * t:64 * t + 64], t == 0, t == 4)
+                return ins
+            op(q, f, ["sg"], [bw])
+        elif kind == "v":
+            op(q, lambda: A.activation(T.ro[:], W[:, 32:40, :], ACT.Identity, bias=3.5, scale=-0.5), [], [bw, "ro"])
+
+    def before(name):
+        kind, c = name[0], name[1]
+        if kind in "wx":
+            return ["g%s%d" % (c, k) for k in range(4)]
+        if kind == "s":
+            return ["r" + c, "d" + c]
+        if kind == "u":
+            return ["t" + c, "b" + c]
+        return {"g": [], "t": [], "a": ["w" + c], "b": ["a" + c], "c": ["b" + c], "d": ["c" + c], "q": ["x" + c],
+                "r": ["q" + c], "v": ["u" + c]}[kind]
+
+    def one_round(orders):
+        done = set()
+        at = {q: 0 for q in orders}
+        while any(at[q] < len(orders[q]) for q in orders):
+            moved = False
+            for q in orders:
+                while at[q] < len(orders[q]) and all(x in done for x in before(orders[q][at[q]])):
+                    step(q, orders[q][at[q]])
+                    done.add(orders[q][at[q]])
+                    at[q] += 1
+                    moved = True
+            assert moved
+
+    combine(1)
+    for t in range(2, R):
+        one_round({"V": ORDER_V, "A": ORDER_A, "P": ORDER_P})
+        combine(t)
+    k = ORDER_A.index("q2") + 1
+    one_round({"V": ORDER_V, "A": ORDER_A[:k] + ["t0"] + ORDER_A[k:] + ["v0"], "P": ORDER_P + ["u0"]})
+
+    wait("G", last_w["ro"])
+    g.remote_dma_fused([RemoteDMATransfer(dst_ids=[dst(u) for u in dests], dma_engine_mask=bits(r_eng), remote_sem=T.sem.ar_r,
+                                          srcs=[T.ro[:]], dsts=[T.rl[:, 64 * rank:64 * rank + 64] for u in dests])],
+                       local_sem=T.sem.loc)
+    loc[0] += len(r_eng)
+    for gl in range(2):
+        p0 = 64 * gl + 16 * rank
+        dma("Y", T.rounds[2 * rank + gl:2 * rank + gl + 1, :], T.ro[p0:p0 + 16, :], "out", reads=["ro"])
+    for q in others:
+        for gl in range(2):
+            p0 = 64 * gl + 16 * rank
+            dma("Y", T.rounds[2 * q + gl:2 * q + gl + 1, :], T.rl[p0:p0 + 16, 64 * q:64 * q + 64], "out",
+                after=[("ar_r", len(r_eng) * len(others), {})])
+
+    FIN = ["fin%d" % w for w in range(4)]
+    for k, u in enumerate(dests + [rank]):
+        def f():
+            for w in range(4):
+                a = BASE + 1024 * u + 256 * w
+                ins = PE.matmul(bank[k][:, 0:256], T.fin[:, 128 * w:128 * w + 128], T.tab[:, a:a + 256], w == 0, w == 3)
+            return ins
+        op("P", f, ["tab"] + FIN, ["B%d" % k])
+    for k, u in enumerate(dests + [rank]):
+        out = T.yo[:, 256 * u:256 * u + 256]
+        if k % 2 == 0:
+            e = op("V", lambda: V.tensor_scalar(out, bank[k][:, 0:256], 3 * U, None, ALU.add), [], ["B%d" % k, "yo%d" % u])
+        else:
+            e = op("A", lambda: A.activation(out, bank[k][:, 0:256], ACT.Identity, bias=3 * U), [], ["B%d" % k, "yo%d" % u])
+        if u != rank:
+            wait("G", e)
+            rid, pid, _ = topo.addr(cores[u])
+            g.remote_dma(T.l_y[rank], out, T.sem["ar_y%d" % rank], T.sem.loc, pid, rid, bits(eng))
+            loc[0] += len(eng)
+    dma("A", T.y[32 * rank:32 * rank + 32, :], T.yo[:, 256 * rank:256 * rank + 256], "out", reads=["yo%d" % rank])
+
+    for k, q in enumerate(sorted(others, key=lambda o: dests_of(o).index(rank))):
+        dma("Y" if k % 2 == 0 else "A", T.y[32 * q:32 * q + 32, :], T.l_y[q], "out", after=[("ar_y%d" % q, len(eng), {})])
+
+    g.wait_ge(T.sem.loc, loc[0])
+    for sem in sorted(total):
+        g.wait_ge(T.sem[sem], total[sem])

@@ -2,63 +2,68 @@ from concourse.bass import DstId, RemoteDMATransfer
 from concourse.mybir import AluOpType as ALU, ActivationFunctionType as ACT
 
 S, P, R = 4096, 1024, 6
-U = 49152.0
-BASE = 6144
+SLOTS = 1136
+BASE = 6400
 HI = BASE + S
-WIN = HI + P
-BIG = 16384.0
+WIN = HI + SLOTS
+BIG = 16384
+U = 40960
+HALF = 2048
+K1 = BASE + 3 * BIG - S
 EDGES = [0, 16, 32, 48, 64]
-PIECES = [(3, 256), (7, 256), (0, 512), (4, 512), (1, 512), (5, 512), (2, 512), (6, 512), (3, 256), (7, 256)]
+PIECES = list(zip([7, 0, 1, 2, 3, 4, 5, 6, 7], [256] + [512] * 7 + [256]))
 
 SCRATCH = {
     "d_nb": ("dram", [4, 128, 64], "int32"),
-    "l_nb": ("dram", [4, 128, 64], "int32"),
     "d_pk": ("dram", [4, 128, 256], "bfloat16"),
-    "l_pk": ("dram", [4, 128, 256], "bfloat16"),
     "l_y": ("dram", [4, 128, 256], "float32"),
-    "nbs": ("sbuf", [128, 256], "int32"),
+    "l_r": ("dram", [4, 128, 64], "float32"),
+    "nbl": ("sbuf", [128, 256], "int32"),
+    "pkl": ("sbuf", [128, 1024], "bfloat16"),
+    "hh": ("sbuf", [128, 16, 16], "float16"),
+    "ee": ("sbuf", [128, 16, 16], "float16"),
+    "hq": ("sbuf", [128, 64, 5], "float16"),
+    "c16": ("sbuf", [128, 320], "bfloat16"),
+    "col": ("sbuf", [128, 4], "float32"),
     "pk": ("sbuf", [128, 1024], "bfloat16"),
     "off": ("sbuf", [128, 256], "uint16"),
     "soff": ("sbuf", [128, 64], "uint16"),
-    "av": ("sbuf", [128, 320], "float32"),
     "mm": ("sbuf", [128, 320], "float32"),
     "lh": ("sbuf", [128, 320], "float32"),
     "zz": ("sbuf", [128, 320], "float32"),
-    "cw": ("sbuf", [128, 160], "bfloat16"),
+    "z1": ("sbuf", [128, 64], "float32"),
+    "hi1": ("sbuf", [128, 64], "float32"),
     "tab": ("sbuf", [128, WIN], "bfloat16"),
     "tt": ("sbuf", [128, S + 16], "bfloat16"),
     "gg": ("sbuf", [128, 1024, 4], "bfloat16"),
     "qq": ("sbuf", [128, 1024], "bfloat16"),
     "rr": ("sbuf", [128, 1024], "bfloat16"),
-    "di": ("sbuf", [128, 128], "int32"),
-    "dj": ("sbuf", [128, 128], "int32"),
-    "dk": ("sbuf", [128, 16], "int32"),
-    "c16": ("sbuf", [128, 64], "float32"),
-    "pmi": ("sbuf", [128, 4], "int32"),
-    "pmj": ("sbuf", [128, 4], "int32"),
-    "pmf": ("sbuf", [128, 4], "float32"),
-    "m16": ("sbuf", [128, 16], "float32"),
+    "vi": ("sbuf", [128, 224], "int32"),
+    "vs": ("sbuf", [128, 224], "int32"),
+    "ek": ("sbuf", [128, 4, 224], "float16"),
+    "es": ("sbuf", [128, 224], "float16"),
+    "ones": ("sbuf", [128, 144], "bfloat16"),
+    "turn": ("sbuf", [128, 128], "bfloat16"),
     "eye": ("sbuf", [128, 128], "bfloat16"),
     "neg": ("sbuf", [128, 128], "bfloat16"),
     "cmb": ("sbuf", [128, 128], "bfloat16"),
-    "sel": ("sbuf", [128, 2048], "bfloat16"),
-    "fin": ("sbuf", [128, 512], "bfloat16"),
+    "one16": ("sbuf", [128, 144], "bfloat16"),
+    "sel": ("sbuf", [128, 144], "bfloat16"),
+    "fin": ("sbuf", [128, 144], "bfloat16"),
     "rt": ("sbuf", [128, 320], "bfloat16"),
     "sg": ("sbuf", [128, 320], "bfloat16"),
     "ro": ("sbuf", [128, 64], "float32"),
-    "rl": ("sbuf", [128, 256], "float32"),
     "yo": ("sbuf", [128, 1024], "float32"),
 }
 for _b in range(8):
     SCRATCH["b%d" % _b] = ("psum", [128, 512] if _b < 4 else [128, 64, 8], "float32")
 
-SEMAPHORES = ["sv", "sa", "sp", "sg", "st_nb", "st_pk", "own_nb", "own_pk", "ar_nb", "ar_pk", "re_nb", "re_pk", "rd",
-              "ar_r", "ar_y0", "ar_y1", "ar_y2", "ar_y3", "loc", "out"]
+SEMAPHORES = ["sv", "sa", "sp", "sg", "st_nb", "st_pk", "own_nb", "own_pk", "ar_nb", "ar_p1", "ar_p2", "ar_p3", "rd",
+              "own_r", "ar_r", "ar_y0", "ar_y1", "ar_y2", "ar_y3", "loc", "out"]
 
-ORDER_V = ["g00", "g02", "g10", "g12", "g20", "g22", "b0", "q0", "c0", "r0", "d0", "b1", "s0", "c1", "r1", "d1", "b2", "s1",
-           "c2", "r2", "d2", "b3", "s2", "c3", "r3", "d3", "s3"]
-ORDER_A = ["g01", "g03", "g11", "g13", "g21", "a0", "g23", "g30", "a1", "g31", "q1", "g32", "a2", "g33", "q2", "a3", "q3"]
-ORDER_P = ["w0", "x0", "w1", "x1", "w2", "x2", "w3", "x3"]
+ORDER_V = "g00 g02 g10 g11 g20 g21 g22 c0 r0 d0 c1 s0 d1 r1 s1 c2 r2 d2 c3 s2 d3 r3 s3".split()
+ORDER_A = "g01 g03 g12 g13 g30 b0 q0 g31 b1 g23 q1 g32 g33 b2 q2 b3 q3".split()
+ORDER_P = "p0 a0 p1 a1 p2 a2 p3 a3 x00 x01 w0 x02 x03 x10 w1 x11 x12 x13 x20 x21 w2 x22 x23 w3 x30 x31 x32 x33".split()
 
 
 def rank_program(g, core, T, topo):
@@ -119,13 +124,15 @@ def rank_program(g, core, T, topo):
     V, A, PE = g.vector, g.scalar, g.tensor
     bank = [T["b%d" % b] for b in range(8)]
 
-    def dests_of(q):
-        o = [u for u in range(n) if u != q]
-        return [u for u in o if topo.die(cores[u]) != topo.die(cores[q])] + \
-               [u for u in o if topo.die(cores[u]) == topo.die(cores[q])]
+    def served(q):
+        near = [u for u in range(n) if topo.die(cores[u]) == topo.die(cores[q])]
+        far = [u for u in range(n) if u not in near]
+        k = near.index(q) % len(far)
+        return [u for u in near if u != q] + far[k:] + far[:k]
 
     others = [u for u in range(n) if u != rank]
-    dests = dests_of(rank)
+    dests = served(rank)
+    assert sorted(served(q).index(rank) for q in others) == list(range(n - 1))
     eng = topo.engines(core, cores[others[0]])
 
     def bits(lst):
@@ -139,133 +146,168 @@ def rank_program(g, core, T, topo):
         return DstId(rid=rid, pnc=pid)
 
     ev_e, od_e = eng[0::2], eng[1::2]
-    nb_eng = [ev_e[0:2], ev_e[2:4], od_e[0:2]]
-    pk_eng = [ev_e[0:2] + ev_e[4:6], ev_e[2:4] + ev_e[6:8], od_e[0:2] + od_e[4:6]]
-    r_eng = od_e[2:4] + od_e[6:8]
+    nb_eng = [od_e[0:4], ev_e[0:4], ev_e[4:8]]
+    pk_eng = [od_e[4:8], ev_e[0:8], od_e[0:4]]
+    r_eng = od_e[4:8]
     loc = [0]
 
-    def arrivals(table):
-        return sum(len(table[dests_of(q).index(rank)]) for q in others)
+    def iota(out, pattern, base, step, name, whole=False):
+        if whole:
+            op("G", lambda: g.iota(out, pattern, base, step), writes=[name])
+        else:
+            op("G", lambda: g.iota(out, pattern, base, step, allow_small_or_imprecise_dtypes=True), writes=[name, "pool"])
+
+    def mark(out, ones, pattern, base, step, name):
+        op("G", lambda: g.affine_select(out, ones, pattern, ALU.is_equal, 0.0, base, step), ["ones"], [name, "pool"])
+
+    def fill(ap, x, name):
+        op("V", lambda: V.memset(ap, x), writes=[name])
+
+    def ts(out, in0, a, b, *ops, r, w):
+        op("V", lambda: V.tensor_scalar(out, in0, a, b, *ops), r, w)
 
     e_st_nb = dma("Y", T.d_nb[:], T.nb[:], "st_nb")
     e_st_pk = dma("A", T.d_pk[:], T.packets[:], "st_pk")
-    e_own_nb = dma("Y", T.l_nb[rank], T.nb[32 * rank:32 * rank + 32, :], "own_nb")
-    e_own_pk = dma("A", T.l_pk[rank], T.packets[32 * rank:32 * rank + 32, :], "own_pk")
+    dma("Y", T.nbl[:, 0:64], T.nb[32 * rank:32 * rank + 32, :], "own_nb", writes=["nb0"])
+    dma("A", T.pkl[:, 0:256], T.packets[32 * rank:32 * rank + 32, :], "own_pk", writes=["pl0"])
 
-    op("G", lambda: g.iota(T.di[:], [[-1, 128]], 128, 1), writes=["di"])
-    op("G", lambda: g.iota(T.c16[:], [[16, 64]], 0, 0, allow_small_or_imprecise_dtypes=True), writes=["c16"])
-    op("G", lambda: g.iota(T.pmi[:], [[0, 4]], 0, 1), writes=["pmi"])
+    fill(T.ones[:], 1.0, "ones")
+    iota(T.vi[:], [[-4, 224]], 384, 1, "vi", True)
+    mark(T.turn[:], T.ones[:, 0:128], [[-1, 4], [-4, 32]], 0, 1, "turn")
+    iota(T.hi1[:], [[16, 64]], HI - K1, 1, "hi1")
 
     wait("G", e_st_nb)
     g.remote_dma_fused([RemoteDMATransfer(dst_ids=[dst(u)], dma_engine_mask=bits(nb_eng[k]), remote_sem=T.sem.ar_nb,
-                                          src=T.d_nb[u], dst=T.l_nb[rank]) for k, u in enumerate(dests)], local_sem=T.sem.loc)
+                                          src=T.d_nb[u], dst=T.nbl[:, 64 * (k + 1):64 * (k + 2)])
+                        for k, u in enumerate(dests)], local_sem=T.sem.loc)
     loc[0] += sum(len(x) for x in nb_eng)
     wait("G", e_st_pk)
-    g.remote_dma_fused([RemoteDMATransfer(dst_ids=[dst(u)], dma_engine_mask=bits(pk_eng[k]), remote_sem=T.sem.ar_pk,
-                                          src=T.d_pk[u], dst=T.l_pk[rank]) for k, u in enumerate(dests)], local_sem=T.sem.loc)
+    g.remote_dma_fused([RemoteDMATransfer(dst_ids=[dst(u)], dma_engine_mask=bits(pk_eng[k]), remote_sem=T.sem["ar_p%d" % (k + 1)],
+                                          src=T.d_pk[u], dst=T.pkl[:, 256 * (k + 1):256 * (k + 2)])
+                        for k, u in enumerate(dests)], local_sem=T.sem.loc)
     loc[0] += sum(len(x) for x in pk_eng)
+    last_w["nb1"] = ("ar_nb", sum(len(x) for x in nb_eng), {})
+    for k in range(1, n):
+        last_w["pl%d" % k] = ("ar_p%d" % k, len(pk_eng[k - 1]), {})
 
-    dma("Y", T.nbs[:], T.l_nb[:], "re_nb", writes=["nbs"], after=[e_own_nb, ("ar_nb", arrivals(nb_eng), {})])
-    dma("A", T.pk[:], T.l_pk[:], "re_pk", writes=["pk"], after=[e_own_pk, ("ar_pk", arrivals(pk_eng), {})])
+    for b in range(4):
+        mark(T.cmb[32 * b:32 * b + 32, :], T.ones[32 * b:32 * b + 32, 0:128], [[0, 4], [-1, 32]], 0, 1, "cmb%d" % b)
+    mark(T.eye[:], T.ones[:, 0:128], [[-1, 128]], 0, 1, "eye")
+    mark(T.one16[:], T.ones[:], [[-16, 9], [1000, 16]], 16, 1, "one16")
+    iota(T.c16[:], [[-16, 64], [0, 5]], 0, 0, "c16")
+    iota(T.col[:], [[0, 4]], BASE + HALF - U, -1, "col")
+    iota(T.lh[:], [[16, 64], [0, 5]], HI, 1, "lh")
+    iota(T.lh[:, 0::5], [[16, 64]], 0, 1, "lh")
+    for b in range(4):
+        mark(T.fin[32 * b:32 * b + 32, :], T.ones[32 * b:32 * b + 32, :], [[-1, 144]], 3, 4, "fin%d" % b)
+    CMB = ["cmb%d" % b for b in range(4)]
+    FIN = ["fin%d" % b for b in range(4)]
 
-    op("V", lambda: V.memset(T.tab[:, BASE:HI], -U), writes=["tab"])
-    op("V", lambda: V.memset(T.tt[:, S:S + 16], 0.0), writes=["ttz"])
-    op("V", lambda: V.memset(T.av[:, 0::5], BIG), writes=["av4"])
-    op("V", lambda: V.memset(bank[1][:, 0:320:5], BIG), writes=["w1_4"])
-    op("V", lambda: V.memset(T.cw[:], 0.0), writes=["cw"])
-    op("V", lambda: V.memset(T.fin[:], 0.0), writes=["fin"])
-    op("V", lambda: V.tensor_scalar(T.eye[:], T.di[:], 128, None, ALU.is_equal), ["di"], ["eye"])
-    op("V", lambda: V.tensor_scalar(T.neg[:], T.di[:], 128, -1.0, ALU.is_equal, ALU.mult), ["di"], ["neg"])
-    op("V", lambda: V.tensor_scalar(T.dj[:], T.di[:], 31, None, ALU.bitwise_and), ["di"], ["dj"])
-    op("V", lambda: V.tensor_scalar(T.dk[:], T.di[:, 0:16], 15, None, ALU.bitwise_and), ["di"], ["dk"])
-    op("V", lambda: V.tensor_scalar(T.pmj[:], T.pmi[:], 15, None, ALU.bitwise_and), ["pmi"], ["pmj"])
-    op("V", lambda: V.memset(T.cw[:, 0::5], -U), writes=["cw"])
-    op("V", lambda: V.tensor_scalar(T.cmb[:], T.dj[:], 0, None, ALU.is_equal), ["dj"], ["cmb"])
-    op("V", lambda: V.tensor_scalar(T.m16[:], T.dk[:], 0, None, ALU.is_equal), ["dk"], ["m16"])
-    op("V", lambda: V.tensor_copy(T.pmf[:], T.pmj[:]), ["pmj"], ["pmf"])
-    for w in range(4):
-        op("V", lambda: V.tensor_copy(T.fin[:, 128 * w + w:128 * w + 128:4], T.cmb[:, 0:32]), ["cmb", "fin"], ["fin%d" % w])
-    op("V", lambda: V.tensor_scalar(T.lh[:, 0::5], T.c16[:], T.pmf[:, 0:1], None, ALU.add), ["c16", "pmf"], ["lh0"])
-    for k in range(1, 5):
-        op("V", lambda: V.tensor_scalar(T.lh[:, k::5], T.c16[:], T.pmf[:, 0:1], float(HI), ALU.add, ALU.add),
-           ["c16", "pmf"], ["lh%d" % k])
-    op("V", lambda: V.tensor_scalar(bank[0][:, 0:64], T.lh[:, 0::5], -1.0, float(BASE), ALU.mult, ALU.add), ["lh0"], ["B0"])
-    for i in range(16):
-        op("V", lambda: V.tensor_scalar(T.sel[:, 128 * i:128 * i + 128], T.eye[:], T.m16[:, i:i + 1], None, ALU.mult),
-           ["eye", "m16"], ["sel%d" % i])
-    LH = ["lh%d" % k for k in range(5)]
-    SEL = ["sel%d" % i for i in range(16)]
+    fill(T.tab[:, BASE:HI], -float(U), "tab")
+    ts(T.vs[:], T.vi[:], 2, None, ALU.arith_shift_right, r=["vi"], w=["vs"])
+    ts(T.ek[:, 0, :], T.vi[:], 0, None, ALU.is_equal, r=["vi"], w=["ek0"])
+    ts(T.es[:], T.vs[:], 0, None, ALU.is_equal, r=["vs"], w=["es"])
+
+    def window(w):
+        return slice(96 - 32 * w, 224 - 32 * w)
+
+    def first_lists(s0, s1, Z, name, bz):
+        ts(T.hh[:, 4 * s0:4 * s1, :], T.nbl[:, 64 * s0:64 * s1], -HALF, None, ALU.add, r=[name], w=["h" + name])
+        ts(T.ee[:, 4 * s0:4 * s1, :], T.nbl[:, 64 * s0:64 * s1], S, -BIG, ALU.is_equal, ALU.mult, r=[name], w=["e" + name])
+
+        def f():
+            for j, src in enumerate([T.hh, T.ee]):
+                for w in range(4):
+                    ins = PE.matmul(Z, T.es[:, window(w)], src[:, 4 * s0 + w:4 * s1:4, :], j + w == 0, j + w == 4)
+            return ins
+        op("P", f, ["h" + name, "e" + name, "es"], [bz])
+
+    def first_offsets(s0, s1, Z, name, bz):
+        cs = slice(16 * s0, 16 * s1)
+        op("V", lambda: V.tensor_tensor(T.z1[:, cs], Z, T.hi1[:, cs], ALU.min), ["hi1"], [bz, "z" + name])
+        ts(T.soff[:, cs], T.z1[:, cs], K1, None, ALU.add, r=["z" + name], w=["s" + name])
+
+    def first_packets(s):
+        cs = slice(256 * s, 256 * s + 256)
+        op("P", lambda: PE.matmul(bank[s][:, 0:256], T.turn[:], T.pkl[:, cs], True, True), ["pl%d" % s, "turn"], ["B%d" % s])
+        op("A", lambda: A.activation(T.pk[:, cs], bank[s][:, 0:256], ACT.Copy), [], ["B%d" % s, "pk%d" % s])
+
+    def first_scatter(s):
+        op("V", lambda: V.tensor_copy(T.tab[:, 0:WIN].indirect(T.soff[:, 16 * s:16 * s + 16]), T.pk[:, 256 * s:256 * s + 256]),
+           ["pk%d" % s, "snb%d" % min(s, 1)], ["tab"])
+
+    first_lists(0, 1, bank[4][:, 0:2, :], "nb0", "B4")
+    first_packets(0)
+    ts(T.ek[:, 1, :], T.vi[:], 1, None, ALU.is_equal, r=["vi"], w=["ek1"])
+    first_offsets(0, 1, bank[4][:, 0:2, :], "nb0", "B4")
+    first_scatter(0)
+    for k in (2, 3):
+        ts(T.ek[:, k, :], T.vi[:], k, None, ALU.is_equal, r=["vi"], w=["ek%d" % k])
+    fill(T.hq[:, :, 0], U + 8192.0, "hq0")
+    fill(T.tt[:, S:S + 16], 0.0, "ttz")
     TT = ["tt%d" % b for b in range(len(PIECES))] + ["ttz"]
-    AV = ["av%d" % k for k in range(5)]
+    PK = ["pk%d" % s for s in range(n)]
+    HH = ["hnb0", "hnb1"] + ["ek%d" % k for k in range(4)]
 
-    for k in range(4):
-        op("V", lambda: V.tensor_scalar(bank[1][:, k + 1:320:5], T.nbs[:, 64 * k:64 * k + 64], -float(S), -BIG, ALU.add, ALU.mult),
-           ["nbs"], ["w1_%d" % k])
-    for k in range(4):
-        op("V", lambda: V.tensor_tensor(T.av[:, k + 1::5], T.nbs[:, 64 * k:64 * k + 64], bank[0][:, 0:64], ALU.add),
-           ["nbs", "B0"], ["av%d" % k])
-    MM = ["mm%d" % c for c in range(4)]
-    op("V", lambda: V.tensor_tensor(T.mm[:], bank[1][:, 0:320], T.av[:], ALU.min),
-       AV + ["w1_%d" % k for k in range(5)], MM + ["B0", "B1"])
-    op("V", lambda: V.tensor_tensor_scan(T.zz[:], T.mm[:], T.lh[:], 0.0, ALU.add, ALU.min), MM + LH,
-       ["zz%d" % c for c in range(4)])
-    op("V", lambda: V.tensor_copy(T.soff[:], T.zz[:, 4::5]), ["zz%d" % c for c in range(4)], ["so%d" % c for c in range(4)])
-    op("V", lambda: V.tensor_copy(T.tab[:, 0:WIN].indirect(T.soff[:, 0:64]), T.pk[:]),
-       ["pk"] + ["so%d" % c for c in range(4)], ["tab"])
-    op("V", lambda: V.tensor_copy(T.off[:], T.nbs[:]), ["nbs"], ["off"])
+    first_lists(1, n, bank[5][:, 0:6, :], "nb1", "B5")
+    first_offsets(1, n, bank[5][:, 0:6, :], "nb1", "B5")
+
+    def lay(out_of):
+        for k in range(4):
+            for w in range(4):
+                ins = PE.matmul(out_of(k), T.ek[:, k, window(w)], T.hh[:, w:16:4, :], w == 0, w == 3)
+        return ins
+
+    op("P", lambda: lay(lambda k: bank[7][:, 8 * k:8 * k + 8, :]), HH, ["B7"])
+    ts(T.off[:], bank[7][:, 0:32, :], HALF, None, ALU.add, r=[], w=["B7", "off"])
+    first_packets(1)
+    first_scatter(1)
+    first_packets(2)
+    op("P", lambda: lay(lambda k: bank[6][:, :, k]), HH, ["B6"])
+    first_scatter(2)
+    first_packets(3)
+    first_scatter(3)
+    op("V", lambda: V.tensor_copy(T.hq[:, :, 1:5], bank[6][:, :, 0:4]), [], ["B6", "hq1"])
+    op("A", lambda: A.activation(T.neg[:], T.eye[:], ACT.Identity, scale=-1.0), ["eye"], ["neg"])
+    op("A", lambda: A.activation(T.sel[:], T.one16[:], ACT.Identity, scale=-1.0), ["one16"], ["sel"])
+    for c in range(len(EDGES) - 1):
+        last_w["so%d" % c] = last_w["tab"]
 
     def combine(t):
-        start = [sum(w for _, w in PIECES[:k]) for k in range(len(PIECES))]
-
-        def region(k):
-            b, w = PIECES[k]
-            return bank[b][:, 0:w] if b < 4 else bank[b][:, 0:w // 8, :]
-
-        def add(k):
-            a = BASE + start[k]
-            op("P", lambda: PE.matmul(region(k), T.cmb[:], T.tab[:, a:a + PIECES[k][1]], True, True),
-               ["tab", "cmb"], ["B%d" % PIECES[k][0]])
-
-        def move(k):
-            out = T.tt[:, start[k]:start[k] + PIECES[k][1]]
+        a = 0
+        for k, (b, w) in enumerate(PIECES):
+            region = bank[b][:, 0:w] if b < 4 else bank[b][:, 0:w // 8, :]
+            op("P", lambda: PE.matmul(region, T.cmb[:], T.tab[:, BASE + a:BASE + a + w], True, True), ["tab"] + CMB, ["B%d" % b])
             if k % 2 == 0:
-                op("V", lambda: V.tensor_scalar(out, region(k), 3 * U, None, ALU.add), [], ["B%d" % PIECES[k][0], "tt%d" % k])
+                op("V", lambda: V.tensor_scalar(T.tt[:, a:a + w], region, 3.0 * U, None, ALU.add), [], ["B%d" % b, "tt%d" % k])
             else:
-                op("A", lambda: A.activation(out, region(k), ACT.Identity, bias=3 * U), [], ["B%d" % PIECES[k][0], "tt%d" % k])
-
-        for k in range(8):
-            add(k)
-        move(0)
-        move(1)
-        add(8)
-        add(9)
-        for k in range(2, 10):
-            move(k)
-        for c in range(4):
-            c0, c1 = EDGES[c], EDGES[c + 1]
-            op("P", lambda: PE.matmul(bank[4 + c][:, 0:c1 - c0, 0:5], T.eye[:], T.cw[:, 0:5 * (c1 - c0)], True, False),
-               ["cw", "eye"], ["B%d" % (4 + c)], inc=0)
-            op("P", lambda: PE.matmul(bank[c][:, 0:16 * (c1 - c0)], T.eye[:], T.pk[:, 16 * c0:16 * c1], True, False),
-               ["pk", "eye"], ["B%d" % c], inc=0)
+                op("A", lambda: A.activation(T.tt[:, a:a + w], region, ACT.Identity, bias=3.0 * U), [], ["B%d" % b, "tt%d" % k])
+            a += w
         for gl in range(2):
             dma("Y", T.rt[64 * gl:64 * gl + 64, 64 * (t - 1):64 * t], T.tt[16 * gl:16 * gl + 1, 0:S], "rd",
-                reads=TT, writes=["rt%d" % gl])
-        both = last_w["rt1"]
-        last_w["rt0"] = both
+                reads=TT, writes=["rt%d_%d" % (t, gl)])
+        both = last_w["rt%d_1" % t]
+        last_w["rt%d_0" % t] = both
         for x in TT:
             readers[x] = [e for e in readers[x] if e[0] != "rd"] + [both]
 
+    def gathers_of(c):
+        return ["g%d%d" % (c, k) for k in range(4)]
+
     def step(q, name):
         kind, c = name[0], int(name[1])
+        if kind == "t":
+            op(q, lambda: A.activation(T.sg[:, 64 * (c - 1):64 * c], T.rt[:, 64 * (c - 1):64 * c], ACT.Sign, bias=0.5),
+               ["rt%d_0" % c, "rt%d_1" % c], ["sg%d" % c])
+            return
         c0, c1 = EDGES[c], EDGES[c + 1]
         m = c1 - c0
         X, W = bank[c][:, 0:16 * m], bank[4 + c]
         bx, bw = "B%d" % c, "B%d" % (4 + c)
-        gc = ["g%d%d" % (c, k) for k in range(4)]
+        gc = gathers_of(c)
         cols = slice(16 * c0, 16 * c1)
         pc = slice(c0, c1)
         p5 = slice(5 * c0, 5 * c1)
-        W5 = W[:, 0:m, 0:5]
         if kind == "g":
             k = int(name[2])
             src = T.tt[:, 0:S + 16].indirect(T.off[:, 64 * k + c0:64 * k + c1])
@@ -273,62 +315,56 @@ def rank_program(g, core, T, topo):
                 op(q, lambda: V.tensor_copy(T.gg[:, cols, k], src), TT + ["off"], [name])
             else:
                 op(q, lambda: A.activation(T.gg[:, cols, k], src, ACT.Copy), TT + ["off"], [name])
+        elif kind == "p":
+            op(q, lambda: PE.matmul(X, T.eye[:], T.pk[:, cols], True, False), PK + ["eye"], [bx], inc=0)
+        elif kind == "a":
+            op(q, lambda: PE.matmul(W[:, 0:m, 0:5], T.eye[:], T.hq[:, pc, :], True, False), ["hq0", "hq1", "eye"], [bw], inc=0)
+            op(q, lambda: PE.matmul(W[:, 0:m, 0:5], T.eye[:], T.c16[:, p5], False, False), ["c16"], [], inc=0)
         elif kind == "w":
             def f():
                 for i in range(16):
-                    ins = PE.matmul(W[:, 0:m, 1:5], T.sel[:, 128 * i:128 * i + 128], T.gg[:, 16 * c0 + i:16 * c1:16, :],
-                                    False, i == 15)
+                    ins = PE.matmul(W[:, 0:m, 1:5], T.sel[:, 16 - i:144 - i], T.gg[:, 16 * c0 + i:16 * c1:16, :], False, i == 15)
                 return ins
-            op(q, f, gc + SEL, [bw])
+            op(q, f, gc + ["sel"], [bw])
         elif kind == "x":
-            def f():
-                for k in range(4):
-                    ins = PE.matmul(X, T.neg[:], T.gg[:, cols, k], False, k == 3)
-                return ins
-            op(q, f, gc + ["neg"], [bx])
-        elif kind == "a":
-            if q == "V":
-                op(q, lambda: V.tensor_scalar(W5, W5, -1.0, 0.0, ALU.mult, ALU.max), [], [bw])
+            k = int(name[2])
+            if k < 3:
+                op(q, lambda: PE.matmul(X, T.neg[:], T.gg[:, cols, k], False, False), [gc[k], "neg"], [], inc=0)
             else:
-                op(q, lambda: A.activation(W5, W5, ACT.Relu, scale=-1.0), [], [bw])
+                op(q, lambda: PE.matmul(X, T.neg[:], T.gg[:, cols, k], False, True), gc + ["neg"], [bx])
         elif kind == "b":
-            op(q, lambda: V.tensor_tensor(T.mm[:, p5], W5, T.av[:, p5], ALU.min), AV, [bw, "mm%d" % c])
+            op(q, lambda: A.activation(T.mm[:, p5], W[:, 0:m, 0:5], ACT.Relu, bias=T.col[:, 0:1]), ["col"], [bw, "mm%d" % c])
         elif kind == "c":
             op(q, lambda: V.tensor_tensor_scan(T.zz[:, p5], T.mm[:, p5], T.lh[:, p5], 0.0, ALU.add, ALU.min),
-               ["mm%d" % c] + LH, ["zz%d" % c])
+               ["mm%d" % c, "lh"], ["zz%d" % c])
         elif kind == "d":
             op(q, lambda: V.tensor_copy(T.soff[:, pc], T.zz[:, 5 * c0 + 4:5 * c1:5]), ["zz%d" % c], ["so%d" % c])
         elif kind == "q":
-            if q == "V":
-                op(q, lambda: V.tensor_scalar(T.qq[:, cols], X, -127.5, None, ALU.add), [], [bx, "q%d" % c])
-            else:
-                op(q, lambda: A.activation(T.qq[:, cols], X, ACT.Identity, bias=-127.5), [], [bx, "q%d" % c])
+            op(q, lambda: A.activation(T.qq[:, cols], X, ACT.Identity, bias=-127.5), [], [bx, "q%d" % c])
         elif kind == "r":
             op(q, lambda: V.tensor_tensor(T.rr[:, cols], X, T.qq[:, cols], ALU.subtract), ["q%d" % c], [bx, "r%d" % c])
         elif kind == "s":
             op(q, lambda: V.tensor_copy(T.tab[:, 0:WIN].indirect(T.soff[:, pc]), T.rr[:, cols]),
                ["r%d" % c, "so%d" % c], ["tab"])
-        elif kind == "t":
-            op(q, lambda: A.activation(T.sg[:], T.rt[:], ACT.Sign, bias=0.5), ["rt0", "rt1"], ["sg"])
         elif kind == "u":
             def f():
                 for t in range(5):
-                    ins = PE.matmul(W[:, 32:40, :], T.eye[:], T.sg[:, 64 * t:64 * t + 64], t == 0, t == 4)
+                    ins = PE.matmul(bank[c][:, 0:64], T.eye[:], T.sg[:, 64 * t:64 * t + 64], t == 0, t == 4)
                 return ins
-            op(q, f, ["sg"], [bw])
+            op(q, f, ["sg%d" % t for t in range(1, 6)], [bx])
         elif kind == "v":
-            op(q, lambda: A.activation(T.ro[:], W[:, 32:40, :], ACT.Identity, bias=3.5, scale=-0.5), [], [bw, "ro"])
+            op(q, lambda: A.activation(T.ro[:], bank[c][:, 0:64], ACT.Identity, bias=3.5, scale=-0.5), [], [bx, "ro"])
 
     def before(name):
         kind, c = name[0], name[1]
-        if kind in "wx":
-            return ["g%s%d" % (c, k) for k in range(4)]
+        if kind == "w":
+            return gathers_of(int(c))
+        if kind == "x":
+            return ["g" + name[1:]]
         if kind == "s":
             return ["r" + c, "d" + c]
-        if kind == "u":
-            return ["t" + c, "b" + c]
-        return {"g": [], "t": [], "a": ["w" + c], "b": ["a" + c], "c": ["b" + c], "d": ["c" + c], "q": ["x" + c],
-                "r": ["q" + c], "v": ["u" + c]}[kind]
+        return {"g": [], "t": [], "p": [], "a": [], "b": ["w" + c], "c": ["b" + c], "d": ["c" + c], "q": ["x" + c + "3"],
+                "r": ["q" + c], "u": ["t5", "r" + c], "v": ["u" + c]}[kind]
 
     def one_round(orders):
         done = set()
@@ -343,50 +379,55 @@ def rank_program(g, core, T, topo):
                     moved = True
             assert moved
 
+    def put(order, name, behind):
+        k = order.index(behind) + 1
+        return order[:k] + [name] + order[k:]
+
     combine(1)
     for t in range(2, R):
-        one_round({"V": ORDER_V, "A": ORDER_A, "P": ORDER_P})
+        one_round({"V": ORDER_V, "A": ORDER_A + ["t%d" % (t - 1)], "P": ORDER_P})
         combine(t)
-    k = ORDER_A.index("q2") + 1
-    one_round({"V": ORDER_V, "A": ORDER_A[:k] + ["t0"] + ORDER_A[k:] + ["v0"], "P": ORDER_P + ["u0"]})
+    one_round({"V": ORDER_V, "A": put(put(ORDER_A, "t5", "q1"), "v0", "q2"), "P": put(ORDER_P, "u0", "x23")})
 
     wait("G", last_w["ro"])
     g.remote_dma_fused([RemoteDMATransfer(dst_ids=[dst(u) for u in dests], dma_engine_mask=bits(r_eng), remote_sem=T.sem.ar_r,
-                                          srcs=[T.ro[:]], dsts=[T.rl[:, 64 * rank:64 * rank + 64] for u in dests])],
+                                          srcs=[T.ro[:]], dsts=[T.l_r[rank] for u in dests])],
                        local_sem=T.sem.loc)
     loc[0] += len(r_eng)
+    e_own_r = dma("Y", T.l_r[rank], T.ro[:], "own_r", reads=["ro"])
     for gl in range(2):
         p0 = 64 * gl + 16 * rank
-        dma("Y", T.rounds[2 * rank + gl:2 * rank + gl + 1, :], T.ro[p0:p0 + 16, :], "out", reads=["ro"])
-    for q in others:
-        for gl in range(2):
-            p0 = 64 * gl + 16 * rank
-            dma("Y", T.rounds[2 * q + gl:2 * q + gl + 1, :], T.rl[p0:p0 + 16, 64 * q:64 * q + 64], "out",
-                after=[("ar_r", len(r_eng) * len(others), {})])
+        dma("Y", T.rounds[gl::2, :], T.l_r[:, p0:p0 + 16, :], "out", after=[e_own_r, ("ar_r", len(r_eng) * len(others), {})])
 
-    FIN = ["fin%d" % w for w in range(4)]
-    for k, u in enumerate(dests + [rank]):
+    turn = dests[1:] + dests[:1]
+    Y_CALLS = [[0], [1], [2]]
+    y_eng = [eng, eng, eng]
+    for k, u in enumerate(turn + [rank]):
         def f():
             for w in range(4):
                 a = BASE + 1024 * u + 256 * w
-                ins = PE.matmul(bank[k][:, 0:256], T.fin[:, 128 * w:128 * w + 128], T.tab[:, a:a + 256], w == 0, w == 3)
+                ins = PE.matmul(bank[k][:, 0:256], T.fin[:, 3 - w:131 - w], T.tab[:, a:a + 256], w == 0, w == 3)
             return ins
         op("P", f, ["tab"] + FIN, ["B%d" % k])
-    for k, u in enumerate(dests + [rank]):
+    for k, u in enumerate(turn + [rank]):
         out = T.yo[:, 256 * u:256 * u + 256]
         if k % 2 == 0:
-            e = op("V", lambda: V.tensor_scalar(out, bank[k][:, 0:256], 3 * U, None, ALU.add), [], ["B%d" % k, "yo%d" % u])
+            e = op("V", lambda: V.tensor_scalar(out, bank[k][:, 0:256], 3.0 * U, None, ALU.add), [], ["B%d" % k, "yo%d" % u])
         else:
-            e = op("A", lambda: A.activation(out, bank[k][:, 0:256], ACT.Identity, bias=3 * U), [], ["B%d" % k, "yo%d" % u])
-        if u != rank:
-            wait("G", e)
-            rid, pid, _ = topo.addr(cores[u])
-            g.remote_dma(T.l_y[rank], out, T.sem["ar_y%d" % rank], T.sem.loc, pid, rid, bits(eng))
-            loc[0] += len(eng)
+            e = op("A", lambda: A.activation(out, bank[k][:, 0:256], ACT.Identity, bias=3.0 * U), [], ["B%d" % k, "yo%d" % u])
+        for call in Y_CALLS:
+            if k == call[-1]:
+                for j in call:
+                    wait("G", last_w["yo%d" % turn[j]])
+                g.remote_dma_fused([RemoteDMATransfer(dst_ids=[dst(turn[j])], dma_engine_mask=bits(y_eng[j]),
+                                                      remote_sem=T.sem["ar_y%d" % rank],
+                                                      src=T.yo[:, 256 * turn[j]:256 * turn[j] + 256], dst=T.l_y[rank])
+                                    for j in call], local_sem=T.sem.loc)
+                loc[0] += sum(len(y_eng[j]) for j in call)
     dma("A", T.y[32 * rank:32 * rank + 32, :], T.yo[:, 256 * rank:256 * rank + 256], "out", reads=["yo%d" % rank])
 
-    for k, q in enumerate(sorted(others, key=lambda o: dests_of(o).index(rank))):
-        dma("Y" if k % 2 == 0 else "A", T.y[32 * q:32 * q + 32, :], T.l_y[q], "out", after=[("ar_y%d" % q, len(eng), {})])
+    for k, q in enumerate(sorted(others, key=lambda o: (served(o).index(rank) - 1) % (n - 1))):
+        dma("Y" if k % 2 == 0 else "A", T.y[32 * q:32 * q + 32, :], T.l_y[q], "out", after=[("ar_y%d" % q, len(y_eng[k]), {})])
 
     g.wait_ge(T.sem.loc, loc[0])
     for sem in sorted(total):

from concourse.bass import DstId, RemoteDMATransfer
from concourse.mybir import AluOpType as ALU, ActivationFunctionType as ACT

S, P, R = 4096, 1024, 6
SLOTS = 1136
BASE = 6400
HI = BASE + S
WIN = HI + SLOTS
BIG = 16384
U = 40960
HALF = 2048
K1 = BASE + 3 * BIG - S
EDGES = [0, 16, 32, 48, 64]
PIECES = list(zip([7, 0, 1, 2, 3, 4, 5, 6, 7], [256] + [512] * 7 + [256]))

SCRATCH = {
    "d_nb": ("dram", [4, 128, 64], "int32"),
    "d_pk": ("dram", [4, 128, 256], "bfloat16"),
    "l_y": ("dram", [4, 128, 256], "float32"),
    "l_r": ("dram", [4, 128, 64], "float32"),
    "nbl": ("sbuf", [128, 256], "int32"),
    "pkl": ("sbuf", [128, 1024], "bfloat16"),
    "hh": ("sbuf", [128, 16, 16], "float16"),
    "ee": ("sbuf", [128, 16, 16], "float16"),
    "hq": ("sbuf", [128, 64, 5], "float16"),
    "c16": ("sbuf", [128, 320], "bfloat16"),
    "col": ("sbuf", [128, 4], "float32"),
    "pk": ("sbuf", [128, 1024], "bfloat16"),
    "off": ("sbuf", [128, 256], "uint16"),
    "soff": ("sbuf", [128, 64], "uint16"),
    "mm": ("sbuf", [128, 320], "float32"),
    "lh": ("sbuf", [128, 320], "float32"),
    "zz": ("sbuf", [128, 320], "float32"),
    "z1": ("sbuf", [128, 64], "float32"),
    "hi1": ("sbuf", [128, 64], "float32"),
    "tab": ("sbuf", [128, WIN], "bfloat16"),
    "tt": ("sbuf", [128, S + 16], "bfloat16"),
    "gg": ("sbuf", [128, 1024, 4], "bfloat16"),
    "qq": ("sbuf", [128, 1024], "bfloat16"),
    "rr": ("sbuf", [128, 1024], "bfloat16"),
    "vi": ("sbuf", [128, 224], "int32"),
    "vs": ("sbuf", [128, 224], "int32"),
    "ek": ("sbuf", [128, 4, 224], "float16"),
    "es": ("sbuf", [128, 224], "float16"),
    "ones": ("sbuf", [128, 144], "bfloat16"),
    "turn": ("sbuf", [128, 128], "bfloat16"),
    "eye": ("sbuf", [128, 128], "bfloat16"),
    "neg": ("sbuf", [128, 128], "bfloat16"),
    "cmb": ("sbuf", [128, 128], "bfloat16"),
    "one16": ("sbuf", [128, 144], "bfloat16"),
    "sel": ("sbuf", [128, 144], "bfloat16"),
    "fin": ("sbuf", [128, 144], "bfloat16"),
    "rt": ("sbuf", [128, 320], "bfloat16"),
    "sg": ("sbuf", [128, 320], "bfloat16"),
    "ro": ("sbuf", [128, 64], "float32"),
    "yo": ("sbuf", [128, 1024], "float32"),
}
for _b in range(8):
    SCRATCH["b%d" % _b] = ("psum", [128, 512] if _b < 4 else [128, 64, 8], "float32")

SEMAPHORES = ["sv", "sa", "sp", "sg", "st_nb", "st_pk", "own_nb", "own_pk", "ar_nb", "ar_p1", "ar_p2", "ar_p3", "rd",
              "own_r", "ar_r", "ar_y0", "ar_y1", "ar_y2", "ar_y3", "loc", "out"]

ORDER_V = "g00 g02 g10 g11 g20 g21 g22 c0 r0 d0 c1 s0 d1 r1 s1 c2 r2 d2 c3 s2 d3 r3 s3".split()
ORDER_A = "g01 g03 g12 g13 g30 b0 q0 g31 b1 g23 q1 g32 g33 b2 q2 b3 q3".split()
ORDER_P = "p0 a0 p1 a1 p2 a2 p3 a3 x00 x01 w0 x02 x03 x10 w1 x11 x12 x13 x20 x21 w2 x22 x23 w3 x30 x31 x32 x33".split()


def rank_program(g, core, T, topo):
    rank = T.rank_of(core)
    if rank is None:
        return
    cores = list(T.cores)
    n = len(cores)
    Q = {"V": g.vector, "A": g.scalar, "P": g.tensor, "G": g, "Y": g.sync}
    own = {"V": "sv", "A": "sa", "P": "sp", "G": "sg"}
    clock = {k: {} for k in Q}
    total = {}
    last_w, readers = {}, {}

    def wait(q, ev):
        sem, cnt, seen = ev
        if clock[q].get(sem, 0) >= cnt:
            return
        Q[q].wait_ge(T.sem[sem], cnt)
        clock[q][sem] = cnt
        for k, v in seen.items():
            if clock[q].get(k, 0) < v:
                clock[q][k] = v

    def deps(reads, writes):
        evs = []
        for x in list(reads) + list(writes):
            if x in last_w:
                evs.append(last_w[x])
        for x in writes:
            evs.extend(readers.get(x, []))
        best = {}
        for e in evs:
            if e[0] not in best or best[e[0]][1] < e[1]:
                best[e[0]] = e
        return sorted(best.values(), key=lambda e: -len(e[2]))

    def op(q, fn, reads=(), writes=(), sem=None, inc=1, after=()):
        for e in list(after) + deps(reads, writes):
            wait(q, e)
        ins = fn()
        if inc == 0:
            return None
        sem = sem or own[q]
        ins.then_inc(T.sem[sem], inc)
        total[sem] = total.get(sem, 0) + inc
        ev = (sem, total[sem], dict(clock[q]))
        for x in reads:
            readers.setdefault(x, []).append(ev)
        for x in writes:
            last_w[x] = ev
            readers[x] = []
        return ev

    def dma(q, out, in_, sem, reads=(), writes=(), after=()):
        return op(q, lambda: Q[q].dma_start(out, in_), reads, writes, sem=sem, inc=16, after=after)

    V, A, PE = g.vector, g.scalar, g.tensor
    bank = [T["b%d" % b] for b in range(8)]

    def served(q):
        near = [u for u in range(n) if topo.die(cores[u]) == topo.die(cores[q])]
        far = [u for u in range(n) if u not in near]
        k = near.index(q) % len(far)
        return [u for u in near if u != q] + far[k:] + far[:k]

    others = [u for u in range(n) if u != rank]
    dests = served(rank)
    assert sorted(served(q).index(rank) for q in others) == list(range(n - 1))
    eng = topo.engines(core, cores[others[0]])

    def bits(lst):
        m = 0
        for e in lst:
            m |= 1 << e
        return m

    def dst(u):
        rid, pid, _ = topo.addr(cores[u])
        return DstId(rid=rid, pnc=pid)

    ev_e, od_e = eng[0::2], eng[1::2]
    nb_eng = [od_e[0:4], ev_e[0:4], ev_e[4:8]]
    pk_eng = [od_e[4:8], ev_e[0:8], od_e[0:4]]
    r_eng = od_e[4:8]
    loc = [0]

    def iota(out, pattern, base, step, name, whole=False):
        if whole:
            op("G", lambda: g.iota(out, pattern, base, step), writes=[name])
        else:
            op("G", lambda: g.iota(out, pattern, base, step, allow_small_or_imprecise_dtypes=True), writes=[name, "pool"])

    def mark(out, ones, pattern, base, step, name):
        op("G", lambda: g.affine_select(out, ones, pattern, ALU.is_equal, 0.0, base, step), ["ones"], [name, "pool"])

    def fill(ap, x, name):
        op("V", lambda: V.memset(ap, x), writes=[name])

    def ts(out, in0, a, b, *ops, r, w):
        op("V", lambda: V.tensor_scalar(out, in0, a, b, *ops), r, w)

    e_st_nb = dma("Y", T.d_nb[:], T.nb[:], "st_nb")
    e_st_pk = dma("A", T.d_pk[:], T.packets[:], "st_pk")
    dma("Y", T.nbl[:, 0:64], T.nb[32 * rank:32 * rank + 32, :], "own_nb", writes=["nb0"])
    dma("A", T.pkl[:, 0:256], T.packets[32 * rank:32 * rank + 32, :], "own_pk", writes=["pl0"])

    fill(T.ones[:], 1.0, "ones")
    iota(T.vi[:], [[-4, 224]], 384, 1, "vi", True)
    mark(T.turn[:], T.ones[:, 0:128], [[-1, 4], [-4, 32]], 0, 1, "turn")
    iota(T.hi1[:], [[16, 64]], HI - K1, 1, "hi1")

    wait("G", e_st_nb)
    g.remote_dma_fused([RemoteDMATransfer(dst_ids=[dst(u)], dma_engine_mask=bits(nb_eng[k]), remote_sem=T.sem.ar_nb,
                                          src=T.d_nb[u], dst=T.nbl[:, 64 * (k + 1):64 * (k + 2)])
                        for k, u in enumerate(dests)], local_sem=T.sem.loc)
    loc[0] += sum(len(x) for x in nb_eng)
    wait("G", e_st_pk)
    g.remote_dma_fused([RemoteDMATransfer(dst_ids=[dst(u)], dma_engine_mask=bits(pk_eng[k]), remote_sem=T.sem["ar_p%d" % (k + 1)],
                                          src=T.d_pk[u], dst=T.pkl[:, 256 * (k + 1):256 * (k + 2)])
                        for k, u in enumerate(dests)], local_sem=T.sem.loc)
    loc[0] += sum(len(x) for x in pk_eng)
    last_w["nb1"] = ("ar_nb", sum(len(x) for x in nb_eng), {})
    for k in range(1, n):
        last_w["pl%d" % k] = ("ar_p%d" % k, len(pk_eng[k - 1]), {})

    for b in range(4):
        mark(T.cmb[32 * b:32 * b + 32, :], T.ones[32 * b:32 * b + 32, 0:128], [[0, 4], [-1, 32]], 0, 1, "cmb%d" % b)
    mark(T.eye[:], T.ones[:, 0:128], [[-1, 128]], 0, 1, "eye")
    mark(T.one16[:], T.ones[:], [[-16, 9], [1000, 16]], 16, 1, "one16")
    iota(T.c16[:], [[-16, 64], [0, 5]], 0, 0, "c16")
    iota(T.col[:], [[0, 4]], BASE + HALF - U, -1, "col")
    iota(T.lh[:], [[16, 64], [0, 5]], HI, 1, "lh")
    iota(T.lh[:, 0::5], [[16, 64]], 0, 1, "lh")
    for b in range(4):
        mark(T.fin[32 * b:32 * b + 32, :], T.ones[32 * b:32 * b + 32, :], [[-1, 144]], 3, 4, "fin%d" % b)
    CMB = ["cmb%d" % b for b in range(4)]
    FIN = ["fin%d" % b for b in range(4)]

    fill(T.tab[:, BASE:HI], -float(U), "tab")
    ts(T.vs[:], T.vi[:], 2, None, ALU.arith_shift_right, r=["vi"], w=["vs"])
    ts(T.ek[:, 0, :], T.vi[:], 0, None, ALU.is_equal, r=["vi"], w=["ek0"])
    ts(T.es[:], T.vs[:], 0, None, ALU.is_equal, r=["vs"], w=["es"])

    def window(w):
        return slice(96 - 32 * w, 224 - 32 * w)

    def first_lists(s0, s1, Z, name, bz):
        ts(T.hh[:, 4 * s0:4 * s1, :], T.nbl[:, 64 * s0:64 * s1], -HALF, None, ALU.add, r=[name], w=["h" + name])
        ts(T.ee[:, 4 * s0:4 * s1, :], T.nbl[:, 64 * s0:64 * s1], S, -BIG, ALU.is_equal, ALU.mult, r=[name], w=["e" + name])

        def f():
            for j, src in enumerate([T.hh, T.ee]):
                for w in range(4):
                    ins = PE.matmul(Z, T.es[:, window(w)], src[:, 4 * s0 + w:4 * s1:4, :], j + w == 0, j + w == 4)
            return ins
        op("P", f, ["h" + name, "e" + name, "es"], [bz])

    def first_offsets(s0, s1, Z, name, bz):
        cs = slice(16 * s0, 16 * s1)
        op("V", lambda: V.tensor_tensor(T.z1[:, cs], Z, T.hi1[:, cs], ALU.min), ["hi1"], [bz, "z" + name])
        ts(T.soff[:, cs], T.z1[:, cs], K1, None, ALU.add, r=["z" + name], w=["s" + name])

    def first_packets(s):
        cs = slice(256 * s, 256 * s + 256)
        op("P", lambda: PE.matmul(bank[s][:, 0:256], T.turn[:], T.pkl[:, cs], True, True), ["pl%d" % s, "turn"], ["B%d" % s])
        op("A", lambda: A.activation(T.pk[:, cs], bank[s][:, 0:256], ACT.Copy), [], ["B%d" % s, "pk%d" % s])

    def first_scatter(s):
        op("V", lambda: V.tensor_copy(T.tab[:, 0:WIN].indirect(T.soff[:, 16 * s:16 * s + 16]), T.pk[:, 256 * s:256 * s + 256]),
           ["pk%d" % s, "snb%d" % min(s, 1)], ["tab"])

    first_lists(0, 1, bank[4][:, 0:2, :], "nb0", "B4")
    first_packets(0)
    ts(T.ek[:, 1, :], T.vi[:], 1, None, ALU.is_equal, r=["vi"], w=["ek1"])
    first_offsets(0, 1, bank[4][:, 0:2, :], "nb0", "B4")
    first_scatter(0)
    for k in (2, 3):
        ts(T.ek[:, k, :], T.vi[:], k, None, ALU.is_equal, r=["vi"], w=["ek%d" % k])
    fill(T.hq[:, :, 0], U + 8192.0, "hq0")
    fill(T.tt[:, S:S + 16], 0.0, "ttz")
    TT = ["tt%d" % b for b in range(len(PIECES))] + ["ttz"]
    PK = ["pk%d" % s for s in range(n)]
    HH = ["hnb0", "hnb1"] + ["ek%d" % k for k in range(4)]

    first_lists(1, n, bank[5][:, 0:6, :], "nb1", "B5")
    first_offsets(1, n, bank[5][:, 0:6, :], "nb1", "B5")

    def lay(out_of):
        for k in range(4):
            for w in range(4):
                ins = PE.matmul(out_of(k), T.ek[:, k, window(w)], T.hh[:, w:16:4, :], w == 0, w == 3)
        return ins

    op("P", lambda: lay(lambda k: bank[7][:, 8 * k:8 * k + 8, :]), HH, ["B7"])
    ts(T.off[:], bank[7][:, 0:32, :], HALF, None, ALU.add, r=[], w=["B7", "off"])
    first_packets(1)
    first_scatter(1)
    first_packets(2)
    op("P", lambda: lay(lambda k: bank[6][:, :, k]), HH, ["B6"])
    first_scatter(2)
    first_packets(3)
    first_scatter(3)
    op("V", lambda: V.tensor_copy(T.hq[:, :, 1:5], bank[6][:, :, 0:4]), [], ["B6", "hq1"])
    op("A", lambda: A.activation(T.neg[:], T.eye[:], ACT.Identity, scale=-1.0), ["eye"], ["neg"])
    op("A", lambda: A.activation(T.sel[:], T.one16[:], ACT.Identity, scale=-1.0), ["one16"], ["sel"])
    for c in range(len(EDGES) - 1):
        last_w["so%d" % c] = last_w["tab"]

    def combine(t):
        a = 0
        for k, (b, w) in enumerate(PIECES):
            region = bank[b][:, 0:w] if b < 4 else bank[b][:, 0:w // 8, :]
            op("P", lambda: PE.matmul(region, T.cmb[:], T.tab[:, BASE + a:BASE + a + w], True, True), ["tab"] + CMB, ["B%d" % b])
            if k % 2 == 0:
                op("V", lambda: V.tensor_scalar(T.tt[:, a:a + w], region, 3.0 * U, None, ALU.add), [], ["B%d" % b, "tt%d" % k])
            else:
                op("A", lambda: A.activation(T.tt[:, a:a + w], region, ACT.Identity, bias=3.0 * U), [], ["B%d" % b, "tt%d" % k])
            a += w
        for gl in range(2):
            dma("Y", T.rt[64 * gl:64 * gl + 64, 64 * (t - 1):64 * t], T.tt[16 * gl:16 * gl + 1, 0:S], "rd",
                reads=TT, writes=["rt%d_%d" % (t, gl)])
        both = last_w["rt%d_1" % t]
        last_w["rt%d_0" % t] = both
        for x in TT:
            readers[x] = [e for e in readers[x] if e[0] != "rd"] + [both]

    def gathers_of(c):
        return ["g%d%d" % (c, k) for k in range(4)]

    def step(q, name):
        kind, c = name[0], int(name[1])
        if kind == "t":
            op(q, lambda: A.activation(T.sg[:, 64 * (c - 1):64 * c], T.rt[:, 64 * (c - 1):64 * c], ACT.Sign, bias=0.5),
               ["rt%d_0" % c, "rt%d_1" % c], ["sg%d" % c])
            return
        c0, c1 = EDGES[c], EDGES[c + 1]
        m = c1 - c0
        X, W = bank[c][:, 0:16 * m], bank[4 + c]
        bx, bw = "B%d" % c, "B%d" % (4 + c)
        gc = gathers_of(c)
        cols = slice(16 * c0, 16 * c1)
        pc = slice(c0, c1)
        p5 = slice(5 * c0, 5 * c1)
        if kind == "g":
            k = int(name[2])
            src = T.tt[:, 0:S + 16].indirect(T.off[:, 64 * k + c0:64 * k + c1])
            if q == "V":
                op(q, lambda: V.tensor_copy(T.gg[:, cols, k], src), TT + ["off"], [name])
            else:
                op(q, lambda: A.activation(T.gg[:, cols, k], src, ACT.Copy), TT + ["off"], [name])
        elif kind == "p":
            op(q, lambda: PE.matmul(X, T.eye[:], T.pk[:, cols], True, False), PK + ["eye"], [bx], inc=0)
        elif kind == "a":
            op(q, lambda: PE.matmul(W[:, 0:m, 0:5], T.eye[:], T.hq[:, pc, :], True, False), ["hq0", "hq1", "eye"], [bw], inc=0)
            op(q, lambda: PE.matmul(W[:, 0:m, 0:5], T.eye[:], T.c16[:, p5], False, False), ["c16"], [], inc=0)
        elif kind == "w":
            def f():
                for i in range(16):
                    ins = PE.matmul(W[:, 0:m, 1:5], T.sel[:, 16 - i:144 - i], T.gg[:, 16 * c0 + i:16 * c1:16, :], False, i == 15)
                return ins
            op(q, f, gc + ["sel"], [bw])
        elif kind == "x":
            k = int(name[2])
            if k < 3:
                op(q, lambda: PE.matmul(X, T.neg[:], T.gg[:, cols, k], False, False), [gc[k], "neg"], [], inc=0)
            else:
                op(q, lambda: PE.matmul(X, T.neg[:], T.gg[:, cols, k], False, True), gc + ["neg"], [bx])
        elif kind == "b":
            op(q, lambda: A.activation(T.mm[:, p5], W[:, 0:m, 0:5], ACT.Relu, bias=T.col[:, 0:1]), ["col"], [bw, "mm%d" % c])
        elif kind == "c":
            op(q, lambda: V.tensor_tensor_scan(T.zz[:, p5], T.mm[:, p5], T.lh[:, p5], 0.0, ALU.add, ALU.min),
               ["mm%d" % c, "lh"], ["zz%d" % c])
        elif kind == "d":
            op(q, lambda: V.tensor_copy(T.soff[:, pc], T.zz[:, 5 * c0 + 4:5 * c1:5]), ["zz%d" % c], ["so%d" % c])
        elif kind == "q":
            op(q, lambda: A.activation(T.qq[:, cols], X, ACT.Identity, bias=-127.5), [], [bx, "q%d" % c])
        elif kind == "r":
            op(q, lambda: V.tensor_tensor(T.rr[:, cols], X, T.qq[:, cols], ALU.subtract), ["q%d" % c], [bx, "r%d" % c])
        elif kind == "s":
            op(q, lambda: V.tensor_copy(T.tab[:, 0:WIN].indirect(T.soff[:, pc]), T.rr[:, cols]),
               ["r%d" % c, "so%d" % c], ["tab"])
        elif kind == "u":
            def f():
                for t in range(5):
                    ins = PE.matmul(bank[c][:, 0:64], T.eye[:], T.sg[:, 64 * t:64 * t + 64], t == 0, t == 4)
                return ins
            op(q, f, ["sg%d" % t for t in range(1, 6)], [bx])
        elif kind == "v":
            op(q, lambda: A.activation(T.ro[:], bank[c][:, 0:64], ACT.Identity, bias=3.5, scale=-0.5), [], [bx, "ro"])

    def before(name):
        kind, c = name[0], name[1]
        if kind == "w":
            return gathers_of(int(c))
        if kind == "x":
            return ["g" + name[1:]]
        if kind == "s":
            return ["r" + c, "d" + c]
        return {"g": [], "t": [], "p": [], "a": [], "b": ["w" + c], "c": ["b" + c], "d": ["c" + c], "q": ["x" + c + "3"],
                "r": ["q" + c], "u": ["t5", "r" + c], "v": ["u" + c]}[kind]

    def one_round(orders):
        done = set()
        at = {q: 0 for q in orders}
        while any(at[q] < len(orders[q]) for q in orders):
            moved = False
            for q in orders:
                while at[q] < len(orders[q]) and all(x in done for x in before(orders[q][at[q]])):
                    step(q, orders[q][at[q]])
                    done.add(orders[q][at[q]])
                    at[q] += 1
                    moved = True
            assert moved

    def put(order, name, behind):
        k = order.index(behind) + 1
        return order[:k] + [name] + order[k:]

    combine(1)
    for t in range(2, R):
        one_round({"V": ORDER_V, "A": ORDER_A + ["t%d" % (t - 1)], "P": ORDER_P})
        combine(t)
    one_round({"V": ORDER_V, "A": put(put(ORDER_A, "t5", "q1"), "v0", "q2"), "P": put(ORDER_P, "u0", "x23")})

    wait("G", last_w["ro"])
    g.remote_dma_fused([RemoteDMATransfer(dst_ids=[dst(u) for u in dests], dma_engine_mask=bits(r_eng), remote_sem=T.sem.ar_r,
                                          srcs=[T.ro[:]], dsts=[T.l_r[rank] for u in dests])],
                       local_sem=T.sem.loc)
    loc[0] += len(r_eng)
    e_own_r = dma("Y", T.l_r[rank], T.ro[:], "own_r", reads=["ro"])
    for gl in range(2):
        p0 = 64 * gl + 16 * rank
        dma("Y", T.rounds[gl::2, :], T.l_r[:, p0:p0 + 16, :], "out", after=[e_own_r, ("ar_r", len(r_eng) * len(others), {})])

    turn = dests[1:] + dests[:1]
    Y_CALLS = [[0], [1], [2]]
    y_eng = [eng, eng, eng]
    for k, u in enumerate(turn + [rank]):
        def f():
            for w in range(4):
                a = BASE + 1024 * u + 256 * w
                ins = PE.matmul(bank[k][:, 0:256], T.fin[:, 3 - w:131 - w], T.tab[:, a:a + 256], w == 0, w == 3)
            return ins
        op("P", f, ["tab"] + FIN, ["B%d" % k])
    for k, u in enumerate(turn + [rank]):
        out = T.yo[:, 256 * u:256 * u + 256]
        if k % 2 == 0:
            e = op("V", lambda: V.tensor_scalar(out, bank[k][:, 0:256], 3.0 * U, None, ALU.add), [], ["B%d" % k, "yo%d" % u])
        else:
            e = op("A", lambda: A.activation(out, bank[k][:, 0:256], ACT.Identity, bias=3.0 * U), [], ["B%d" % k, "yo%d" % u])
        for call in Y_CALLS:
            if k == call[-1]:
                for j in call:
                    wait("G", last_w["yo%d" % turn[j]])
                g.remote_dma_fused([RemoteDMATransfer(dst_ids=[dst(turn[j])], dma_engine_mask=bits(y_eng[j]),
                                                      remote_sem=T.sem["ar_y%d" % rank],
                                                      src=T.yo[:, 256 * turn[j]:256 * turn[j] + 256], dst=T.l_y[rank])
                                    for j in call], local_sem=T.sem.loc)
                loc[0] += sum(len(y_eng[j]) for j in call)
    dma("A", T.y[32 * rank:32 * rank + 32, :], T.yo[:, 256 * rank:256 * rank + 256], "out", reads=["yo%d" % rank])

    for k, q in enumerate(sorted(others, key=lambda o: (served(o).index(rank) - 1) % (n - 1))):
        dma("Y" if k % 2 == 0 else "A", T.y[32 * q:32 * q + 32, :], T.l_y[q], "out", after=[("ar_y%d" % q, len(y_eng[k]), {})])

    g.wait_ge(T.sem.loc, loc[0])
    for sem in sorted(total):
        g.wait_ge(T.sem[sem], total[sem])
